import numpy as np
import ml_dtypes


def mxq(x, axis, fmt="e4m3"):
    dtype, down = {"e4m3": (ml_dtypes.float8_e4m3fn, 7), "e5m2": (ml_dtypes.float8_e5m2, 14)}[fmt]
    v = np.moveaxis(np.asarray(x, np.float32).astype(ml_dtypes.bfloat16).astype(np.float64), axis, -1)
    blocks = v.reshape(v.shape[:-1] + (-1, 32))
    amax = np.abs(blocks).max(-1, keepdims=True)
    byte = np.maximum(np.where(amax > 0, np.frexp(amax)[1] - 1 + 127, 0) - down, 1)
    scale = np.exp2(byte - 127.0)
    codes = (blocks / scale).astype(np.float32).astype(dtype).astype(np.float64)
    return np.moveaxis((codes * scale).reshape(v.shape), -1, axis)


WIDE = False


def mx_kscale(k):
    if not WIDE:
        return np.ones(k)
    levels = np.array([10, -10, 5, -5, 0])
    if k % 512:
        return np.exp2(np.random.permutation(np.resize(levels, k // 32))).repeat(32)
    a = np.empty((k // 512, 16))
    for p in range(k // 512):
        a[p, :8] = np.random.permutation(np.resize(levels, 8))
        for g in range(8):
            far = levels[np.abs(levels - a[p, g]) >= 10]
            a[p, g + 8] = far[np.random.randint(len(far))]
    return np.exp2(a.ravel()).repeat(32)


def f64(x):
    return np.asarray(x).astype(np.float64)


def striped(idx):
    return np.tile(idx.reshape(-1, 16).T, (8, 1)).astype(np.uint16)


def unstriped(offs):
    return offs[:16].T.reshape(-1).astype(np.int64)


def relu(v):
    return np.maximum(v, 0.0)


K, T, E, C, H, N = 1024, 512, 6, 256, 512, 256
TOP = 3


def by_expert(wq, xq):
    return np.concatenate([wq[e].T @ xq[:, e * C:(e + 1) * C] for e in range(E)], axis=1)


def setup_inputs():
    n = np.random.standard_normal
    s = mx_kscale(K)[:, None]
    u = mx_kscale(H)
    deal = np.repeat(np.arange(E), C).reshape(TOP, T)[:, np.random.permutation(T)]
    deal = np.take_along_axis(deal, np.argsort(np.random.rand(TOP, T), axis=0), axis=0)
    for _ in range(8):
        s_, t_ = np.random.permutation(T).reshape(2, -1); r = np.random.randint(TOP, size=T // 2); x, y = deal[r, s_].copy(), deal[r, t_].copy()
        ok = ~((deal[:, s_] == y).any(0) | (deal[:, t_] == x).any(0)); deal[r[ok], s_[ok]] = y[ok]; deal[r[ok], t_[ok]] = x[ok]
    order = np.lexsort((np.random.rand(TOP * T), deal.reshape(-1)))
    slot_token = order % T; pos = np.empty(TOP * T, np.int64); pos[order] = np.arange(TOP * T); pos = pos.reshape(TOP, T)
    g = np.random.uniform(0.5, 1.5, (TOP, T)); g = g / g.sum(0)
    return {
        "xT": (n((K, T)) * s).astype(np.float32),
        "w1": (n((E, K, H)) / np.sqrt(K) / s[None]).astype(np.float32),
        "w3": (n((E, K, H)) / np.sqrt(K) / s[None] * u[None, None, :]).astype(np.float32),
        "w2": (n((E, H, N)) / np.sqrt(H) / u[None, :, None]).astype(np.float32),
        "gate": np.stack([np.tile(r, (N, 1)) for r in g]).astype(np.float32),
        "offs": striped(slot_token),
        "pos1": striped(pos[0]),
        "pos2": striped(pos[1]),
        "pos3": striped(pos[2]),
    }


def reference(xT, w1, w3, w2, gate, offs, pos1, pos2, pos3):
    idx = unstriped(offs)
    xq = mxq(f64(xT)[:, idx], 0, "e4m3")
    h = relu(by_expert(mxq(f64(w1), 1, "e4m3"), xq))
    h = h * by_expert(mxq(f64(w3), 1, "e4m3"), xq)
    y = by_expert(mxq(f64(w2), 1, "e4m3"), mxq(h, 0, "e4m3"))
    return sum(f64(gate[r]) * y[:, unstriped(p)] for r, p in enumerate((pos1, pos2, pos3)))

@@ -1,0 +1,281 @@
+from contextlib import ExitStack
+
+import concourse.mybir as mybir
+
+K, T, E, C, H, N = 1024, 512, 6, 256, 512, 256
+TOP = 3
+SLOTS = E * C
+P = 128
+PACK = 4
+PASSES = K // (P * PACK)
+FLOPS = 2 * SLOTS * (2 * K * H + H * N)
+
+F32 = mybir.dt.float32
+BF16 = mybir.dt.bfloat16
+U32 = mybir.dt.uint32
+U16 = mybir.dt.uint16
+U8 = mybir.dt.uint8
+FP8X4 = mybir.dt.float8_e4m3fn_x4
+MULT = mybir.AluOpType.mult
+ADD = mybir.AluOpType.add
+RELU = mybir.ActivationFunctionType.Relu
+
+AHEAD = 7
+GATHER = 384
+VEC_M = {("w1", 0): 0, ("w1", 1): 128, ("w3", 0): 0, ("w3", 1): 32, ("x", 0): 64, ("x", 1): 88, ("w2", 0): 64}
+LATE_W2 = 4
+SPLIT = {("w3", E - 1)}
+
+
+def tile_moe_tk_glu_relu_kernel(tc, xT, w1, w3, w2, gate, offs, pos1, pos2, pos3, out):
+    nc = tc.nc
+    with ExitStack() as ctx:
+        keep = ctx.enter_context(tc.tile_pool(name="keep", bufs=1))
+        raws = ctx.enter_context(tc.tile_pool(name="raws", bufs=9))
+        raws2 = ctx.enter_context(tc.tile_pool(name="raws2", bufs=4))
+        groups = ctx.enter_context(tc.tile_pool(name="groups", bufs=3))
+        codes = ctx.enter_context(tc.tile_pool(name="codes", bufs=4))
+        codes2 = ctx.enter_context(tc.tile_pool(name="codes2", bufs=6))
+        hidden = ctx.enter_context(tc.tile_pool(name="hidden", bufs=6))
+        psum = ctx.enter_context(tc.psum_pool(name="psum", bufs=3))
+        psum_y = ctx.enter_context(tc.psum_pool(name="psum_y", bufs=2))
+
+        offs_sb = keep.tile([P, SLOTS // 16], U16, name="offs_sb")
+        nc.sync.dma_start(offs_sb[:], offs)
+        pos_sb = []
+        for r in range(TOP):
+            pos_tile = keep.tile([P, T // 16], U16, name=f"pos_sb{r}")
+            pos_sb.append(pos_tile)
+
+        x_codes = [keep.tile([P, T], U32, name=f"x_codes{p}", align_bytes=64) for p in range(PASSES)]
+        x_scales = keep.tile([P, T], U8, name="x_scales", align_bytes=64)
+        slot_codes = [keep.tile([P, SLOTS], U32, name=f"slot_codes{p}", align_bytes=64) for p in range(PASSES)]
+        slot_scales = keep.tile([P, SLOTS], U8, name="slot_scales", align_bytes=64)
+        y_sb = [keep.tile([P, SLOTS], F32, name=f"y_sb{n}") for n in range(2)]
+        gate_sb = [[keep.tile([P, T], F32, name=f"gate_sb{n}_{r}") for r in range(TOP)] for n in range(2)]
+        nc.gpsimd.memset(x_scales[:], 0)
+
+        early = E - LATE_W2
+        jobs = [("x", 0, p) for p in range(PASSES)]
+        for e in range(E):
+            jobs += [("w1", e, p) for p in range(PASSES)]
+            jobs += [("w3", e, p) for p in range(PASSES)]
+            if e < early:
+                jobs.append(("w2", e, 0))
+        jobs += [("w2", e, 0) for e in range(early, E)]
+
+        raw = {}
+
+        def load(job):
+            kind, e, p = job
+            if kind == "w2":
+                tile = raws2.tile([P, PACK, N], F32, name="raw2")
+                rows = w2[e]
+            else:
+                tile = raws.tile([P, PACK, 512], F32, name="raw")
+                rows = {"x": xT, "w1": w1[e], "w3": w3[e]}[kind][p * 512 : (p + 1) * 512, :]
+            nc.sync.dma_start(out=tile[:], in_=rows.rearrange("(p j) w -> p j w", j=PACK))
+            raw[job] = tile
+
+        grouped = {}
+
+        def group(job):
+            kind = job[0]
+            tile = raw.pop(job)
+            e, p = job[1:]
+            if kind == "w2":
+                dst_tile = groups.tile([P, PACK * N], BF16, name="grouped2", align_bytes=64)
+                dst = dst_tile[:].rearrange("p (m i j) -> p m j i", i=4, j=PACK)
+            else:
+                if p == 0:
+                    dst_tile = groups.tile([P, PASSES, PACK * 512], BF16, name="grouped", align_bytes=64)
+                else:
+                    dst_tile = grouped[(kind, e, 0)]
+                if kind == "x":
+                    dst = dst_tile[:, p, :].rearrange("p (m i j) -> p m j i", i=4, j=PACK)
+                else:
+                    dst = dst_tile[:, p, :].rearrange("p (i m j) -> p m j i", i=4, j=PACK)
+            src = tile[:].rearrange("p j (m i) -> p m j i", i=4)
+            cut = VEC_M.get((kind, e, p), VEC_M[(kind, p)])
+            width = src.shape[1]
+            if cut > 0:
+                nc.vector.tensor_copy(out=dst[:, :cut], in_=src[:, :cut])
+            if cut < width:
+                nc.scalar.copy(out=dst[:, cut:], in_=src[:, cut:])
+            grouped[job] = dst_tile
+
+        ready = {}
+
+        def quantise(job):
+            kind, e, p = job
+            dst_tile = grouped[job]
+            if kind == "x":
+                scales = x_scales[:] if p == 0 else x_scales[4 * p : P, :]
+                nc.vector.quantize_mx(out=x_codes[p][:].bitcast(FP8X4), scales=scales, in_=dst_tile[:, p, :])
+                return
+            if kind == "w2":
+                c_tile = codes2.tile([P, N], U32, name="c2", align_bytes=64)
+                s_tile = codes2.tile([P, N], U8, name="s2", align_bytes=64)
+                nc.vector.quantize_mx(out=c_tile[:].bitcast(FP8X4), scales=s_tile[:], in_=dst_tile[:])
+                ready[job] = (c_tile[:], s_tile[:])
+                return
+            whole = (kind, e) not in SPLIT
+            if p == 0:
+                c_tile = codes.tile([P, PASSES, 512], U32, name="c1", align_bytes=64)
+                s_tile = codes.tile([P, PASSES, 512], U8, name="s1", align_bytes=64)
+                ready[job] = (c_tile[:, 0, :], s_tile[:, 0, :])
+                ready[(kind, e, 1)] = (c_tile[:, 1, :], s_tile[:, 1, :])
+            if whole and p == 1:
+                c_tile, s_tile = whole_tiles[(kind, e)]
+                nc.vector.quantize_mx(
+                    out=c_tile[:].rearrange("p s w -> p (s w)").bitcast(FP8X4),
+                    scales=s_tile[:].rearrange("p s w -> p (s w)"),
+                    in_=dst_tile[:].rearrange("p s w -> p (s w)"),
+                )
+            elif not whole:
+                c_tile, s_tile = ready[job]
+                nc.vector.quantize_mx(out=c_tile.bitcast(FP8X4), scales=s_tile, in_=dst_tile[:, p, :])
+            elif p == 0:
+                whole_tiles[(kind, e)] = (c_tile, s_tile)
+
+        whole_tiles = {}
+
+        def gather(g):
+            cols = slice(g * GATHER, (g + 1) * GATHER)
+            lst = offs_sb[:, g * GATHER // 16 : (g + 1) * GATHER // 16]
+            for p in range(PASSES):
+                nc.vector.tensor_copy(slot_codes[p][:, cols], x_codes[p][:].indirect(lst))
+            nc.vector.tensor_copy(slot_scales[:, cols], x_scales[:].indirect(lst))
+
+        def first_product(kind, e):
+            banks = []
+            for half in range(2):
+                bank = psum.tile([P, PACK, P], F32, name="bank_a" if kind == "w1" else "bank_b")
+                cols = slice(e * C + half * P, e * C + (half + 1) * P)
+                for t in range(PACK):
+                    for p in range(PASSES):
+                        c_tile, s_tile = ready[(kind, e, p)]
+                        nc.tensor.matmul_mx(
+                            out=bank[:, t, :],
+                            lhsT=c_tile[:, t * P : (t + 1) * P].bitcast(FP8X4),
+                            lhsT_scale=s_tile[:, t * P : (t + 1) * P],
+                            rhs=slot_codes[p][:, cols].bitcast(FP8X4),
+                            rhs_scale=slot_scales[4 * p : P, cols],
+                            start=(p == 0),
+                            stop=(p == PASSES - 1),
+                        )
+                banks.append(bank)
+            return banks
+
+        a_banks, b_banks, a_relu, h_bf, h_ready = {}, {}, {}, {}, {}
+
+        def relu(e):
+            a_relu[e] = []
+            for half in range(2):
+                tile = hidden.tile([P, P, PACK], F32, name="a_relu", bufs=3)
+                nc.scalar.activation(tile[:], a_banks[e][half][:].rearrange("p t n -> p n t"), RELU)
+                a_relu[e].append(tile)
+
+        def gated(e):
+            tile = hidden.tile([P, C, PACK], BF16, name="h_bf", align_bytes=64, bufs=2)
+            for half in range(2):
+                nc.vector.tensor_tensor(
+                    tile[:, half * P : (half + 1) * P, :],
+                    b_banks[e][half][:].rearrange("p t n -> p n t"),
+                    a_relu[e][half][:],
+                    MULT,
+                )
+            h_bf[e] = tile
+
+        def quantise_hidden(e):
+            c_tile = hidden.tile([P, C], U32, name="h_codes", align_bytes=64)
+            s_tile = hidden.tile([P, C], U8, name="h_scales", align_bytes=64)
+            nc.vector.quantize_mx(
+                out=c_tile[:].bitcast(FP8X4), scales=s_tile[:], in_=h_bf[e][:].rearrange("p n t -> p (n t)")
+            )
+            h_ready[e] = (c_tile, s_tile)
+
+        def second_product(e):
+            c_tile, s_tile = ready[("w2", e, 0)]
+            hc, hs = h_ready[e]
+            bank = psum_y.tile([P, 2, C], F32, name="bank_y")
+            for n in range(2):
+                nc.tensor.matmul_mx(
+                    out=bank[:, n, :],
+                    lhsT=c_tile[:, n * P : (n + 1) * P].bitcast(FP8X4),
+                    lhsT_scale=s_tile[:, n * P : (n + 1) * P],
+                    rhs=hc[:].bitcast(FP8X4),
+                    rhs_scale=hs[:],
+                    start=True,
+                    stop=True,
+                )
+            y_banks[e] = bank
+
+        y_banks = {}
+
+        def copy_y(e):
+            for n in range(2):
+                nc.scalar.copy(out=y_sb[n][:, e * C : (e + 1) * C], in_=y_banks[e][:, n, :])
+
+        plan = {}
+
+        def later(step, fn, *args):
+            plan.setdefault(step, []).append((fn, args))
+
+        gather_step = {0: 3, 1: 4, 2: 9, 3: 13}
+        for g, step in gather_step.items():
+            later(step, gather, g)
+
+        def after_quantise(step, job):
+            kind, e, p = job
+            if kind == "w1" and p == 1:
+                a_banks[e] = first_product("w1", e)
+                later(step + 1, relu, e)
+            if kind == "w3" and p == 1:
+                b_banks[e] = first_product("w3", e)
+                later(step + 1, gated, e)
+                later(step + 2, quantise_hidden, e)
+                later(step + 2, finish, e, step + 2)
+            if kind == "w2":
+                later(step, finish, e, step)
+
+        done = []
+
+        def finish(e, step):
+            if e in h_ready and ("w2", e, 0) in ready and e not in done:
+                done.append(e)
+                second_product(e)
+                later(step + 1, copy_y, e)
+
+        total = len(jobs)
+        loaded = 0
+        for step in range(total + 6):
+            while loaded < min(step + AHEAD + 1, total):
+                load(jobs[loaded])
+                loaded += 1
+                if loaded == 6:
+                    for r, pos in enumerate((pos1, pos2, pos3)):
+                        nc.sync.dma_start(pos_sb[r][:], pos)
+                if loaded == total:
+                    for n in range(2):
+                        for r in range(TOP):
+                            nc.sync.dma_start(out=gate_sb[n][r][:], in_=gate[r, n * P : (n + 1) * P, :])
+            if step < total:
+                group(jobs[step])
+            if 1 <= step <= total:
+                quantise(jobs[step - 1])
+                after_quantise(step, jobs[step - 1])
+            for fn, args in plan.get(step, []):
+                fn(*args)
+
+        for n in range(2):
+            parts = []
+            for r in range(TOP):
+                tile = keep.tile([P, T], F32, name=f"part{n}_{r}")
+                nc.vector.tensor_tensor(tile[:], y_sb[n][:].indirect(pos_sb[r][:]), gate_sb[n][r][:], MULT)
+                parts.append(tile)
+            total01 = keep.tile([P, T], F32, name=f"total01_{n}")
+            nc.vector.tensor_tensor(total01[:], parts[0][:], parts[1][:], ADD)
+            result = keep.tile([P, T], F32, name=f"result{n}")
+            nc.vector.tensor_tensor(result[:], total01[:], parts[2][:], ADD)
+            nc.sync.dma_start(out=out[n * P : (n + 1) * P, :], in_=result[:])

@@ -18,13 +18,15 @@ U8 = mybir.dt.uint8
 FP8X4 = mybir.dt.float8_e4m3fn_x4
 MULT = mybir.AluOpType.mult
 ADD = mybir.AluOpType.add
+MAX = mybir.AluOpType.max
 RELU = mybir.ActivationFunctionType.Relu
 
 AHEAD = 7
-GATHER = 384
-VEC_M = {("w1", 0): 0, ("w1", 1): 128, ("w3", 0): 0, ("w3", 1): 32, ("x", 0): 64, ("x", 1): 88, ("w2", 0): 64}
-LATE_W2 = 4
+VEC_M = {("w1", 0): 0, ("w1", 1): 80, ("w3", 0): 0, ("w3", 1): 80, ("x", 0): 64, ("x", 1): 88, ("w2", 0): 0}
+VEC_OVER = {("w2", 3, 0): 0, ("w2", 4, 0): 0, ("w2", 5, 0): 64, ("w3", 5, 0): 64}
+LATE_W2 = 3
 SPLIT = {("w3", E - 1)}
+GATHER_STEP = {0: 3, 1: 5, 2: 9, 3: 13, 4: 17, 5: 21}
 
 
 def tile_moe_tk_glu_relu_kernel(tc, xT, w1, w3, w2, gate, offs, pos1, pos2, pos3, out):
@@ -36,9 +38,10 @@ def tile_moe_tk_glu_relu_kernel(tc, xT, w1, w3, w2, gate, offs, pos1, pos2, pos3
         groups = ctx.enter_context(tc.tile_pool(name="groups", bufs=3))
         codes = ctx.enter_context(tc.tile_pool(name="codes", bufs=4))
         codes2 = ctx.enter_context(tc.tile_pool(name="codes2", bufs=6))
+        slots = ctx.enter_context(tc.tile_pool(name="slots", bufs=3))
         hidden = ctx.enter_context(tc.tile_pool(name="hidden", bufs=6))
-        psum = ctx.enter_context(tc.psum_pool(name="psum", bufs=3))
-        psum_y = ctx.enter_context(tc.psum_pool(name="psum_y", bufs=2))
+        psum = ctx.enter_context(tc.psum_pool(name="psum", bufs=2))
+        psum_y = ctx.enter_context(tc.psum_pool(name="psum_y", bufs=4))
 
         offs_sb = keep.tile([P, SLOTS // 16], U16, name="offs_sb")
         nc.sync.dma_start(offs_sb[:], offs)
@@ -49,22 +52,20 @@ def tile_moe_tk_glu_relu_kernel(tc, xT, w1, w3, w2, gate, offs, pos1, pos2, pos3
 
         x_codes = [keep.tile([P, T], U32, name=f"x_codes{p}", align_bytes=64) for p in range(PASSES)]
         x_scales = keep.tile([P, T], U8, name="x_scales", align_bytes=64)
-        slot_codes = [keep.tile([P, SLOTS], U32, name=f"slot_codes{p}", align_bytes=64) for p in range(PASSES)]
-        slot_scales = keep.tile([P, SLOTS], U8, name="slot_scales", align_bytes=64)
         y_sb = [keep.tile([P, SLOTS], F32, name=f"y_sb{n}") for n in range(2)]
         gate_sb = [[keep.tile([P, T], F32, name=f"gate_sb{n}_{r}") for r in range(TOP)] for n in range(2)]
         nc.gpsimd.memset(x_scales[:], 0)
 
-        early = E - LATE_W2
         jobs = [("x", 0, p) for p in range(PASSES)]
         for e in range(E):
             jobs += [("w1", e, p) for p in range(PASSES)]
             jobs += [("w3", e, p) for p in range(PASSES)]
-            if e < early:
+            if e < 3:
                 jobs.append(("w2", e, 0))
-        jobs += [("w2", e, 0) for e in range(early, E)]
+        jobs += [("w2", e, 0) for e in range(3, E)]
 
-        raw = {}
+        raw, grouped, ready, whole_tiles = {}, {}, {}, {}
+        loads = []
 
         def load(job):
             kind, e, p = job
@@ -74,15 +75,15 @@ def tile_moe_tk_glu_relu_kernel(tc, xT, w1, w3, w2, gate, offs, pos1, pos2, pos3
             else:
                 tile = raws.tile([P, PACK, 512], F32, name="raw")
                 rows = {"x": xT, "w1": w1[e], "w3": w3[e]}[kind][p * 512 : (p + 1) * 512, :]
-            nc.sync.dma_start(out=tile[:], in_=rows.rearrange("(p j) w -> p j w", j=PACK))
+            queues = (nc.sync,)
+            queue = queues[len(loads) % len(queues)]
+            loads.append(job)
+            queue.dma_start(out=tile[:], in_=rows.rearrange("(p j) w -> p j w", j=PACK))
             raw[job] = tile
 
-        grouped = {}
-
         def group(job):
-            kind = job[0]
+            kind, e, p = job
             tile = raw.pop(job)
-            e, p = job[1:]
             if kind == "w2":
                 dst_tile = groups.tile([P, PACK * N], BF16, name="grouped2", align_bytes=64)
                 dst = dst_tile[:].rearrange("p (m i j) -> p m j i", i=4, j=PACK)
@@ -96,15 +97,29 @@ def tile_moe_tk_glu_relu_kernel(tc, xT, w1, w3, w2, gate, offs, pos1, pos2, pos3
                 else:
                     dst = dst_tile[:, p, :].rearrange("p (i m j) -> p m j i", i=4, j=PACK)
             src = tile[:].rearrange("p j (m i) -> p m j i", i=4)
-            cut = VEC_M.get((kind, e, p), VEC_M[(kind, p)])
+            if kind == "w3" and p == 1:
+                moved[e] = []
+                for half in range(2):
+                    hold = hidden.tile([P, P, PACK], F32, name="moved", bufs=3)
+                    nc.scalar.copy(hold[:, 0, 0:1], tile[:, 0, 0:1])
+                    moved[e].append(hold)
+            if kind == "w3" and p == 1 and 0 < e <= 3:
+                for n in range(2):
+                    nc.scalar.copy(y_sb[n][:, (e - 1) * C : (e - 1) * C + 1], tile[:, 0, 0:1])
+            if kind == "w2" and e == E - 1:
+                for late_e in range(3, E - 1):
+                    for n in range(2):
+                        nc.scalar.copy(y_sb[n][:, late_e * C : late_e * C + 1], tile[:, 0, 0:1])
+            if kind == "w1" and p == 1 and e > 0:
+                h_bf[e - 1] = hidden.tile([P, C, PACK], BF16, name="h_bf", align_bytes=64, bufs=2)
+                nc.scalar.copy(h_bf[e - 1][:, 0, 0:2], tile[:, 0, 0:2])
+            cut = VEC_OVER.get((kind, e, p), VEC_M[(kind, p)])
             width = src.shape[1]
             if cut > 0:
                 nc.vector.tensor_copy(out=dst[:, :cut], in_=src[:, :cut])
             if cut < width:
                 nc.scalar.copy(out=dst[:, cut:], in_=src[:, cut:])
             grouped[job] = dst_tile
-
-        ready = {}
 
         def quantise(job):
             kind, e, p = job
@@ -119,39 +134,42 @@ def tile_moe_tk_glu_relu_kernel(tc, xT, w1, w3, w2, gate, offs, pos1, pos2, pos3
                 nc.vector.quantize_mx(out=c_tile[:].bitcast(FP8X4), scales=s_tile[:], in_=dst_tile[:])
                 ready[job] = (c_tile[:], s_tile[:])
                 return
-            whole = (kind, e) not in SPLIT
             if p == 0:
                 c_tile = codes.tile([P, PASSES, 512], U32, name="c1", align_bytes=64)
                 s_tile = codes.tile([P, PASSES, 512], U8, name="s1", align_bytes=64)
-                ready[job] = (c_tile[:, 0, :], s_tile[:, 0, :])
-                ready[(kind, e, 1)] = (c_tile[:, 1, :], s_tile[:, 1, :])
-            if whole and p == 1:
-                c_tile, s_tile = whole_tiles[(kind, e)]
+                whole_tiles[(kind, e)] = (c_tile, s_tile)
+            c_tile, s_tile = whole_tiles[(kind, e)]
+            ready[job] = (c_tile[:, p, :], s_tile[:, p, :])
+            if (kind, e) in SPLIT:
+                nc.vector.quantize_mx(
+                    out=c_tile[:, p, :].bitcast(FP8X4), scales=s_tile[:, p, :], in_=dst_tile[:, p, :]
+                )
+            elif p == 1:
                 nc.vector.quantize_mx(
                     out=c_tile[:].rearrange("p s w -> p (s w)").bitcast(FP8X4),
                     scales=s_tile[:].rearrange("p s w -> p (s w)"),
                     in_=dst_tile[:].rearrange("p s w -> p (s w)"),
                 )
-            elif not whole:
-                c_tile, s_tile = ready[job]
-                nc.vector.quantize_mx(out=c_tile.bitcast(FP8X4), scales=s_tile, in_=dst_tile[:, p, :])
-            elif p == 0:
-                whole_tiles[(kind, e)] = (c_tile, s_tile)
 
-        whole_tiles = {}
+        slot_tiles = {}
 
-        def gather(g):
-            cols = slice(g * GATHER, (g + 1) * GATHER)
-            lst = offs_sb[:, g * GATHER // 16 : (g + 1) * GATHER // 16]
+        def gather(e):
+            lst = offs_sb[:, e * C // 16 : (e + 1) * C // 16]
+            words = []
             for p in range(PASSES):
-                nc.vector.tensor_copy(slot_codes[p][:, cols], x_codes[p][:].indirect(lst))
-            nc.vector.tensor_copy(slot_scales[:, cols], x_scales[:].indirect(lst))
+                tile = slots.tile([P, C], U32, name=f"slot_codes{p}", align_bytes=64)
+                nc.vector.tensor_copy(tile[:], x_codes[p][:].indirect(lst))
+                words.append(tile)
+            tile = slots.tile([P, C], U8, name="slot_scales", align_bytes=64)
+            nc.vector.tensor_copy(tile[:], x_scales[:].indirect(lst))
+            slot_tiles[e] = (words, tile)
 
         def first_product(kind, e):
             banks = []
+            words, scales = slot_tiles[e]
             for half in range(2):
                 bank = psum.tile([P, PACK, P], F32, name="bank_a" if kind == "w1" else "bank_b")
-                cols = slice(e * C + half * P, e * C + (half + 1) * P)
+                cols = slice(half * P, (half + 1) * P)
                 for t in range(PACK):
                     for p in range(PASSES):
                         c_tile, s_tile = ready[(kind, e, p)]
@@ -159,30 +177,38 @@ def tile_moe_tk_glu_relu_kernel(tc, xT, w1, w3, w2, gate, offs, pos1, pos2, pos3
                             out=bank[:, t, :],
                             lhsT=c_tile[:, t * P : (t + 1) * P].bitcast(FP8X4),
                             lhsT_scale=s_tile[:, t * P : (t + 1) * P],
-                            rhs=slot_codes[p][:, cols].bitcast(FP8X4),
-                            rhs_scale=slot_scales[4 * p : P, cols],
+                            rhs=words[p][:, cols].bitcast(FP8X4),
+                            rhs_scale=scales[4 * p : P, cols],
                             start=(p == 0),
                             stop=(p == PASSES - 1),
                         )
                 banks.append(bank)
             return banks
 
-        a_banks, b_banks, a_relu, h_bf, h_ready = {}, {}, {}, {}, {}
+        a_banks, b_banks, moved, h_bf, h_ready, y_banks = {}, {}, {}, {}, {}, {}
 
-        def relu(e):
-            a_relu[e] = []
+        def move_a(e):
             for half in range(2):
-                tile = hidden.tile([P, P, PACK], F32, name="a_relu", bufs=3)
+                tile = moved[e][half]
                 nc.scalar.activation(tile[:], a_banks[e][half][:].rearrange("p t n -> p n t"), RELU)
-                a_relu[e].append(tile)
+
+        def move_b(e):
+            moved[e] = []
+            for half in range(2):
+                tile = hidden.tile([P, P, PACK], F32, name="moved", bufs=3)
+                nc.scalar.copy(tile[:], b_banks[e][half][:].rearrange("p t n -> p n t"))
+                moved[e].append(tile)
 
         def gated(e):
-            tile = hidden.tile([P, C, PACK], BF16, name="h_bf", align_bytes=64, bufs=2)
+            if e in h_bf:
+                tile = h_bf[e]
+            else:
+                tile = hidden.tile([P, C, PACK], BF16, name="h_bf", align_bytes=64, bufs=2)
             for half in range(2):
                 nc.vector.tensor_tensor(
                     tile[:, half * P : (half + 1) * P, :],
                     b_banks[e][half][:].rearrange("p t n -> p n t"),
-                    a_relu[e][half][:],
+                    moved[e][half][:],
                     MULT,
                 )
             h_bf[e] = tile
@@ -211,8 +237,6 @@ def tile_moe_tk_glu_relu_kernel(tc, xT, w1, w3, w2, gate, offs, pos1, pos2, pos3
                 )
             y_banks[e] = bank
 
-        y_banks = {}
-
         def copy_y(e):
             for n in range(2):
                 nc.scalar.copy(out=y_sb[n][:, e * C : (e + 1) * C], in_=y_banks[e][:, n, :])
@@ -222,34 +246,42 @@ def tile_moe_tk_glu_relu_kernel(tc, xT, w1, w3, w2, gate, offs, pos1, pos2, pos3
         def later(step, fn, *args):
             plan.setdefault(step, []).append((fn, args))
 
-        gather_step = {0: 3, 1: 4, 2: 9, 3: 13}
-        for g, step in gather_step.items():
+        for g, step in GATHER_STEP.items():
             later(step, gather, g)
 
         def after_quantise(step, job):
             kind, e, p = job
             if kind == "w1" and p == 1:
                 a_banks[e] = first_product("w1", e)
-                later(step + 1, relu, e)
             if kind == "w3" and p == 1:
+                move_a(e)
+                while held_y:
+                    copy_y(held_y.pop(0))
                 b_banks[e] = first_product("w3", e)
-                later(step + 1, gated, e)
+                later(step + 2, gated, e)
                 later(step + 2, quantise_hidden, e)
                 later(step + 2, finish, e, step + 2)
             if kind == "w2":
                 later(step, finish, e, step)
 
-        done = []
+        done, held_y, late_y = [], [], []
 
         def finish(e, step):
             if e in h_ready and ("w2", e, 0) in ready and e not in done:
                 done.append(e)
                 second_product(e)
-                later(step + 1, copy_y, e)
+                if e < 3 and e < E - 1:
+                    held_y.append(e)
+                elif e < E - 1:
+                    late_y.append(e)
+                else:
+                    while late_y:
+                        copy_y(late_y.pop(0))
+                    later(step + 1, copy_y, e)
 
         total = len(jobs)
         loaded = 0
-        for step in range(total + 6):
+        for step in range(total + 8):
             while loaded < min(step + AHEAD + 1, total):
                 load(jobs[loaded])
                 loaded += 1
@@ -262,7 +294,7 @@ def tile_moe_tk_glu_relu_kernel(tc, xT, w1, w3, w2, gate, offs, pos1, pos2, pos3
                             nc.sync.dma_start(out=gate_sb[n][r][:], in_=gate[r, n * P : (n + 1) * P, :])
             if step < total:
                 group(jobs[step])
-            if 1 <= step <= total:
+            if 1 <= step < total + 1:
                 quantise(jobs[step - 1])
                 after_quantise(step, jobs[step - 1])
             for fn, args in plan.get(step, []):

@@ -22,9 +22,9 @@ MAX = mybir.AluOpType.max
 RELU = mybir.ActivationFunctionType.Relu
 
 AHEAD = 7
-VEC_M = {("w1", 0): 0, ("w1", 1): 80, ("w3", 0): 0, ("w3", 1): 80, ("x", 0): 64, ("x", 1): 88, ("w2", 0): 0}
-VEC_OVER = {("w2", 3, 0): 0, ("w2", 4, 0): 0, ("w2", 5, 0): 64, ("w3", 5, 0): 64}
-LATE_W2 = 3
+VEC_M = {("w1", 0): 0, ("w1", 1): 128, ("w3", 0): 0, ("w3", 1): 128, ("x", 0): 64, ("x", 1): 0, ("w2", 0): 64}
+VEC_OVER = {("w2", 2, 0): 0, ("w2", 3, 0): 0, ("w2", 4, 0): 0, ("w2", 5, 0): 64, ("w3", 5, 0): 32, ("w3", 5, 1): 128}
+LATE_W2 = 4
 SPLIT = {("w3", E - 1)}
 GATHER_STEP = {0: 3, 1: 5, 2: 9, 3: 13, 4: 17, 5: 21}
 
@@ -38,7 +38,7 @@ def tile_moe_tk_glu_relu_kernel(tc, xT, w1, w3, w2, gate, offs, pos1, pos2, pos3
         groups = ctx.enter_context(tc.tile_pool(name="groups", bufs=3))
         codes = ctx.enter_context(tc.tile_pool(name="codes", bufs=4))
         codes2 = ctx.enter_context(tc.tile_pool(name="codes2", bufs=6))
-        slots = ctx.enter_context(tc.tile_pool(name="slots", bufs=3))
+        slots = ctx.enter_context(tc.tile_pool(name="slots", bufs=6))
         hidden = ctx.enter_context(tc.tile_pool(name="hidden", bufs=6))
         psum = ctx.enter_context(tc.psum_pool(name="psum", bufs=2))
         psum_y = ctx.enter_context(tc.psum_pool(name="psum_y", bufs=4))
@@ -60,9 +60,9 @@ def tile_moe_tk_glu_relu_kernel(tc, xT, w1, w3, w2, gate, offs, pos1, pos2, pos3
         for e in range(E):
             jobs += [("w1", e, p) for p in range(PASSES)]
             jobs += [("w3", e, p) for p in range(PASSES)]
-            if e < 3:
+            if e < 2:
                 jobs.append(("w2", e, 0))
-        jobs += [("w2", e, 0) for e in range(3, E)]
+        jobs += [("w2", e, 0) for e in range(2, E)]
 
         raw, grouped, ready, whole_tiles = {}, {}, {}, {}
         loads = []
@@ -97,22 +97,9 @@ def tile_moe_tk_glu_relu_kernel(tc, xT, w1, w3, w2, gate, offs, pos1, pos2, pos3
                 else:
                     dst = dst_tile[:, p, :].rearrange("p (i m j) -> p m j i", i=4, j=PACK)
             src = tile[:].rearrange("p j (m i) -> p m j i", i=4)
-            if kind == "w3" and p == 1:
-                moved[e] = []
-                for half in range(2):
-                    hold = hidden.tile([P, P, PACK], F32, name="moved", bufs=3)
-                    nc.scalar.copy(hold[:, 0, 0:1], tile[:, 0, 0:1])
-                    moved[e].append(hold)
-            if kind == "w3" and p == 1 and 0 < e <= 3:
-                for n in range(2):
-                    nc.scalar.copy(y_sb[n][:, (e - 1) * C : (e - 1) * C + 1], tile[:, 0, 0:1])
-            if kind == "w2" and e == E - 1:
-                for late_e in range(3, E - 1):
-                    for n in range(2):
-                        nc.scalar.copy(y_sb[n][:, late_e * C : late_e * C + 1], tile[:, 0, 0:1])
             if kind == "w1" and p == 1 and e > 0:
                 h_bf[e - 1] = hidden.tile([P, C, PACK], BF16, name="h_bf", align_bytes=64, bufs=2)
-                nc.scalar.copy(h_bf[e - 1][:, 0, 0:2], tile[:, 0, 0:2])
+                nc.vector.tensor_copy(h_bf[e - 1][:, 0:C:P, 0:2], tile[:, 0:2, 0:2])
             cut = VEC_OVER.get((kind, e, p), VEC_M[(kind, p)])
             width = src.shape[1]
             if cut > 0:
@@ -120,6 +107,17 @@ def tile_moe_tk_glu_relu_kernel(tc, xT, w1, w3, w2, gate, offs, pos1, pos2, pos3
             if cut < width:
                 nc.scalar.copy(out=dst[:, cut:], in_=src[:, cut:])
             grouped[job] = dst_tile
+            if kind == "w3" and p == 1:
+                hold = hidden.tile([P, 2, P, PACK], F32, name="moved", bufs=2)
+                nc.scalar.copy(hold[:, :, 0, 0], tile[:, 0:2, 0])
+                moved[e] = [hold[:, half, :, :] for half in range(2)]
+            if kind == "w3" and p == 1 and 0 < e <= 2:
+                for n in range(2):
+                    nc.scalar.copy(y_sb[n][:, (e - 1) * C : (e - 1) * C + 1], tile[:, 0, 0:1])
+            if kind == "w2" and e == E - 1:
+                for late_e in range(2, E - 1):
+                    for n in range(2):
+                        nc.scalar.copy(y_sb[n][:, late_e * C : late_e * C + 1], tile[:, 0, 0:1])
 
         def quantise(job):
             kind, e, p = job
@@ -190,7 +188,7 @@ def tile_moe_tk_glu_relu_kernel(tc, xT, w1, w3, w2, gate, offs, pos1, pos2, pos3
         def move_a(e):
             for half in range(2):
                 tile = moved[e][half]
-                nc.scalar.activation(tile[:], a_banks[e][half][:].rearrange("p t n -> p n t"), RELU)
+                nc.scalar.activation(tile, a_banks[e][half][:].rearrange("p t n -> p n t"), RELU)
 
         def move_b(e):
             moved[e] = []
@@ -208,7 +206,7 @@ def tile_moe_tk_glu_relu_kernel(tc, xT, w1, w3, w2, gate, offs, pos1, pos2, pos3
                 nc.vector.tensor_tensor(
                     tile[:, half * P : (half + 1) * P, :],
                     b_banks[e][half][:].rearrange("p t n -> p n t"),
-                    moved[e][half][:],
+                    moved[e][half],
                     MULT,
                 )
             h_bf[e] = tile
@@ -270,7 +268,7 @@ def tile_moe_tk_glu_relu_kernel(tc, xT, w1, w3, w2, gate, offs, pos1, pos2, pos3
             if e in h_ready and ("w2", e, 0) in ready and e not in done:
                 done.append(e)
                 second_product(e)
-                if e < 3 and e < E - 1:
+                if e < 2 and e < E - 1:
                     held_y.append(e)
                 elif e < E - 1:
                     late_y.append(e)

@@ -5,9 +5,6 @@ import concourse.mybir as mybir
 K, T, E, C, H, N = 1024, 512, 6, 256, 512, 256
 TOP = 3
 SLOTS = E * C
-P = 128
-PACK = 4
-PASSES = K // (P * PACK)
 FLOPS = 2 * SLOTS * (2 * K * H + H * N)
 
 F32 = mybir.dt.float32
@@ -18,294 +15,304 @@ U8 = mybir.dt.uint8
 FP8X4 = mybir.dt.float8_e4m3fn_x4
 MULT = mybir.AluOpType.mult
 ADD = mybir.AluOpType.add
-MAX = mybir.AluOpType.max
 RELU = mybir.ActivationFunctionType.Relu
 
+P = 128
+PACK = 4
+PASS = P * PACK
+PASSES = K // PASS
+HALVES = 2
+QUAD = 4
+SCALE_STEP = 4
+
 AHEAD = 7
-VEC_M = {("w1", 0): 0, ("w1", 1): 128, ("w3", 0): 0, ("w3", 1): 128, ("x", 0): 64, ("x", 1): 0, ("w2", 0): 64}
-VEC_OVER = {("w2", 2, 0): 0, ("w2", 3, 0): 0, ("w2", 4, 0): 0, ("w2", 5, 0): 64, ("w3", 5, 0): 32, ("w3", 5, 1): 128}
-LATE_W2 = 4
-SPLIT = {("w3", E - 1)}
-GATHER_STEP = {0: 3, 1: 5, 2: 9, 3: 13, 4: 17, 5: 21}
+RAW_BUFS = AHEAD + 2
+EARLY_W2 = 2
+LATE = range(EARLY_W2, E)
+LAST = E - 1
+X_QUADS_ON_VECTOR = 64
+LAST_W3_QUADS_ON_VECTOR = 32
+
+
+def chunk_order():
+    order = [("x", 0, s) for s in range(PASSES)]
+    for e in range(E):
+        order += [(kind, e, s) for kind in ("w1", "w3") for s in range(PASSES)]
+        if e < EARLY_W2:
+            order.append(("w2", e, 0))
+    return order + [("w2", e, 0) for e in LATE]
+
+
+def quads_on_vector(kind, e, s):
+    if kind == "x":
+        return X_QUADS_ON_VECTOR if s == 0 else 0
+    if kind == "w2":
+        return N // QUAD if e < EARLY_W2 or e == LAST else 0
+    if s == 1:
+        return H // QUAD
+    return LAST_W3_QUADS_ON_VECTOR if (kind, e) == ("w3", LAST) else 0
 
 
 def tile_moe_tk_glu_relu_kernel(tc, xT, w1, w3, w2, gate, offs, pos1, pos2, pos3, out):
     nc = tc.nc
     with ExitStack() as ctx:
         keep = ctx.enter_context(tc.tile_pool(name="keep", bufs=1))
-        raws = ctx.enter_context(tc.tile_pool(name="raws", bufs=9))
+        raws = ctx.enter_context(tc.tile_pool(name="raws", bufs=RAW_BUFS))
         raws2 = ctx.enter_context(tc.tile_pool(name="raws2", bufs=4))
         groups = ctx.enter_context(tc.tile_pool(name="groups", bufs=3))
         codes = ctx.enter_context(tc.tile_pool(name="codes", bufs=4))
-        codes2 = ctx.enter_context(tc.tile_pool(name="codes2", bufs=6))
-        slots = ctx.enter_context(tc.tile_pool(name="slots", bufs=6))
-        hidden = ctx.enter_context(tc.tile_pool(name="hidden", bufs=6))
-        psum = ctx.enter_context(tc.psum_pool(name="psum", bufs=2))
+        codes2 = ctx.enter_context(tc.tile_pool(name="codes2", bufs=E))
+        slots = ctx.enter_context(tc.tile_pool(name="slots", bufs=E))
+        hidden = ctx.enter_context(tc.tile_pool(name="hidden", bufs=2))
+        hidden_codes = ctx.enter_context(tc.tile_pool(name="hidden_codes", bufs=E))
+        psum = ctx.enter_context(tc.psum_pool(name="psum", bufs=HALVES))
         psum_y = ctx.enter_context(tc.psum_pool(name="psum_y", bufs=4))
 
         offs_sb = keep.tile([P, SLOTS // 16], U16, name="offs_sb")
-        nc.sync.dma_start(offs_sb[:], offs)
-        pos_sb = []
-        for r in range(TOP):
-            pos_tile = keep.tile([P, T // 16], U16, name=f"pos_sb{r}")
-            pos_sb.append(pos_tile)
-
-        x_codes = [keep.tile([P, T], U32, name=f"x_codes{p}", align_bytes=64) for p in range(PASSES)]
+        pos_sb = [keep.tile([P, T // 16], U16, name=f"pos_sb{r}") for r in range(TOP)]
+        x_codes = [keep.tile([P, T], U32, name=f"x_codes{s}", align_bytes=64) for s in range(PASSES)]
         x_scales = keep.tile([P, T], U8, name="x_scales", align_bytes=64)
-        y_sb = [keep.tile([P, SLOTS], F32, name=f"y_sb{n}") for n in range(2)]
-        gate_sb = [[keep.tile([P, T], F32, name=f"gate_sb{n}_{r}") for r in range(TOP)] for n in range(2)]
         nc.gpsimd.memset(x_scales[:], 0)
+        y_sb = [keep.tile([P, SLOTS], F32, name=f"y_sb{n}") for n in range(HALVES)]
+        gate_sb = [keep.tile([P, TOP, T], F32, name=f"gate_sb{n}") for n in range(HALVES)]
 
-        jobs = [("x", 0, p) for p in range(PASSES)]
-        for e in range(E):
-            jobs += [("w1", e, p) for p in range(PASSES)]
-            jobs += [("w3", e, p) for p in range(PASSES)]
-            if e < 2:
-                jobs.append(("w2", e, 0))
-        jobs += [("w2", e, 0) for e in range(2, E)]
+        chunks = chunk_order()
+        raw, grouped, packed = {}, {}, {}
+        slot_codes, relu_a, h_bf, h_packed = {}, {}, {}, {}
+        a_banks, b_banks, y_banks = {}, {}, {}
 
-        raw, grouped, ready, whole_tiles = {}, {}, {}, {}
-        loads = []
-
-        def load(job):
-            kind, e, p = job
+        def load(chunk):
+            kind, e, s = chunk
             if kind == "w2":
                 tile = raws2.tile([P, PACK, N], F32, name="raw2")
                 rows = w2[e]
             else:
-                tile = raws.tile([P, PACK, 512], F32, name="raw")
-                rows = {"x": xT, "w1": w1[e], "w3": w3[e]}[kind][p * 512 : (p + 1) * 512, :]
-            queues = (nc.sync,)
-            queue = queues[len(loads) % len(queues)]
-            loads.append(job)
-            queue.dma_start(out=tile[:], in_=rows.rearrange("(p j) w -> p j w", j=PACK))
-            raw[job] = tile
+                tile = raws.tile([P, PACK, PASS], F32, name="raw")
+                rows = {"x": xT, "w1": w1[e], "w3": w3[e]}[kind][s * PASS : (s + 1) * PASS, :]
+            nc.sync.dma_start(out=tile[:], in_=rows.rearrange("(p j) w -> p j w", j=PACK))
+            raw[chunk] = tile
 
-        def group(job):
-            kind, e, p = job
-            tile = raw.pop(job)
+        def interleave(chunk):
+            kind, e, s = chunk
+            tile = raw.pop(chunk)
             if kind == "w2":
-                dst_tile = groups.tile([P, PACK * N], BF16, name="grouped2", align_bytes=64)
-                dst = dst_tile[:].rearrange("p (m i j) -> p m j i", i=4, j=PACK)
+                target = groups.tile([P, PACK * N], BF16, name="grouped2", align_bytes=64)
+                flat = target[:]
             else:
-                if p == 0:
-                    dst_tile = groups.tile([P, PASSES, PACK * 512], BF16, name="grouped", align_bytes=64)
+                if s == 0:
+                    target = groups.tile([P, PASSES, PACK * PASS], BF16, name="grouped", align_bytes=64)
                 else:
-                    dst_tile = grouped[(kind, e, 0)]
-                if kind == "x":
-                    dst = dst_tile[:, p, :].rearrange("p (m i j) -> p m j i", i=4, j=PACK)
-                else:
-                    dst = dst_tile[:, p, :].rearrange("p (i m j) -> p m j i", i=4, j=PACK)
-            src = tile[:].rearrange("p j (m i) -> p m j i", i=4)
-            if kind == "w1" and p == 1 and e > 0:
-                h_bf[e - 1] = hidden.tile([P, C, PACK], BF16, name="h_bf", align_bytes=64, bufs=2)
-                nc.vector.tensor_copy(h_bf[e - 1][:, 0:C:P, 0:2], tile[:, 0:2, 0:2])
-            cut = VEC_OVER.get((kind, e, p), VEC_M[(kind, p)])
-            width = src.shape[1]
-            if cut > 0:
-                nc.vector.tensor_copy(out=dst[:, :cut], in_=src[:, :cut])
-            if cut < width:
-                nc.scalar.copy(out=dst[:, cut:], in_=src[:, cut:])
-            grouped[job] = dst_tile
-            if kind == "w3" and p == 1:
-                hold = hidden.tile([P, 2, P, PACK], F32, name="moved", bufs=2)
-                nc.scalar.copy(hold[:, :, 0, 0], tile[:, 0:2, 0])
-                moved[e] = [hold[:, half, :, :] for half in range(2)]
-            if kind == "w3" and p == 1 and 0 < e <= 2:
-                for n in range(2):
-                    nc.scalar.copy(y_sb[n][:, (e - 1) * C : (e - 1) * C + 1], tile[:, 0, 0:1])
-            if kind == "w2" and e == E - 1:
-                for late_e in range(2, E - 1):
-                    for n in range(2):
-                        nc.scalar.copy(y_sb[n][:, late_e * C : late_e * C + 1], tile[:, 0, 0:1])
+                    target = grouped[kind, e, 0]
+                flat = target[:, s, :]
+            grouped[chunk] = target
+            source = tile[:].rearrange("p j (m i) -> p m j i", i=QUAD)
+            if kind in ("w1", "w3"):
+                flat = flat.rearrange("p (i m j) -> p m j i", i=QUAD, j=PACK)
+            else:
+                flat = flat.rearrange("p (m i j) -> p m j i", i=QUAD, j=PACK)
 
-        def quantise(job):
-            kind, e, p = job
-            dst_tile = grouped[job]
+            if kind == "w1" and s == 1 and e > 0:
+                h_bf[e - 1] = hidden.tile([P, C, PACK], BF16, name="h_bf", align_bytes=64)
+                nc.vector.tensor_copy(h_bf[e - 1][:, 0:C:P, 0:2], tile[:, 0:2, 0:2])
+            cut = quads_on_vector(kind, e, s)
+            if cut > 0:
+                nc.vector.tensor_copy(out=flat[:, :cut], in_=source[:, :cut])
+            if cut < source.shape[1]:
+                nc.scalar.copy(out=flat[:, cut:], in_=source[:, cut:])
+            if kind == "w3" and s == 1:
+                relu_a[e] = hidden.tile([P, HALVES, P, PACK], F32, name="relu_a")
+                nc.scalar.copy(relu_a[e][:, :, 0, 0], tile[:, 0:HALVES, 0])
+                if 1 <= e <= EARLY_W2:
+                    for n in range(HALVES):
+                        nc.scalar.copy(y_sb[n][:, (e - 1) * C : (e - 1) * C + 1], tile[:, 0, 0:1])
+            if chunk == chunks[-1]:
+                nc.scalar.copy(y_sb[0][:, LATE[0] * C : LAST * C : C], tile[:, 0, 0 : LAST - LATE[0]])
+
+        def quantise(chunk):
+            kind, e, s = chunk
+            source = grouped[chunk]
             if kind == "x":
-                scales = x_scales[:] if p == 0 else x_scales[4 * p : P, :]
-                nc.vector.quantize_mx(out=x_codes[p][:].bitcast(FP8X4), scales=scales, in_=dst_tile[:, p, :])
+                nc.vector.quantize_mx(
+                    out=x_codes[s][:].bitcast(FP8X4), scales=x_scales[SCALE_STEP * s : P, :], in_=source[:, s, :]
+                )
                 return
             if kind == "w2":
-                c_tile = codes2.tile([P, N], U32, name="c2", align_bytes=64)
-                s_tile = codes2.tile([P, N], U8, name="s2", align_bytes=64)
-                nc.vector.quantize_mx(out=c_tile[:].bitcast(FP8X4), scales=s_tile[:], in_=dst_tile[:])
-                ready[job] = (c_tile[:], s_tile[:])
+                words = codes2.tile([P, N], U32, name="w2_codes", align_bytes=64)
+                scales = codes2.tile([P, N], U8, name="w2_scales", align_bytes=64)
+                nc.vector.quantize_mx(out=words[:].bitcast(FP8X4), scales=scales[:], in_=source[:])
+                packed[kind, e] = (words, scales)
                 return
-            if p == 0:
-                c_tile = codes.tile([P, PASSES, 512], U32, name="c1", align_bytes=64)
-                s_tile = codes.tile([P, PASSES, 512], U8, name="s1", align_bytes=64)
-                whole_tiles[(kind, e)] = (c_tile, s_tile)
-            c_tile, s_tile = whole_tiles[(kind, e)]
-            ready[job] = (c_tile[:, p, :], s_tile[:, p, :])
-            if (kind, e) in SPLIT:
+            if s == 0:
+                words = codes.tile([P, PASSES, H], U32, name="w_codes", align_bytes=64)
+                scales = codes.tile([P, PASSES, H], U8, name="w_scales", align_bytes=64)
+                packed[kind, e] = (words, scales)
+            words, scales = packed[kind, e]
+            if (kind, e) == ("w3", LAST):
+                nc.vector.quantize_mx(out=words[:, s, :].bitcast(FP8X4), scales=scales[:, s, :], in_=source[:, s, :])
+            elif s == PASSES - 1:
                 nc.vector.quantize_mx(
-                    out=c_tile[:, p, :].bitcast(FP8X4), scales=s_tile[:, p, :], in_=dst_tile[:, p, :]
-                )
-            elif p == 1:
-                nc.vector.quantize_mx(
-                    out=c_tile[:].rearrange("p s w -> p (s w)").bitcast(FP8X4),
-                    scales=s_tile[:].rearrange("p s w -> p (s w)"),
-                    in_=dst_tile[:].rearrange("p s w -> p (s w)"),
+                    out=words[:].rearrange("p s w -> p (s w)").bitcast(FP8X4),
+                    scales=scales[:].rearrange("p s w -> p (s w)"),
+                    in_=source[:].rearrange("p s w -> p (s w)"),
                 )
 
-        slot_tiles = {}
-
-        def gather(e):
-            lst = offs_sb[:, e * C // 16 : (e + 1) * C // 16]
+        def gather_tokens(e):
+            entries = offs_sb[:, e * C // 16 : (e + 1) * C // 16]
             words = []
-            for p in range(PASSES):
-                tile = slots.tile([P, C], U32, name=f"slot_codes{p}", align_bytes=64)
-                nc.vector.tensor_copy(tile[:], x_codes[p][:].indirect(lst))
+            for s in range(PASSES):
+                tile = slots.tile([P, C], U32, name=f"slot_codes{s}", align_bytes=64)
+                nc.vector.tensor_copy(tile[:], x_codes[s][:].indirect(entries))
                 words.append(tile)
-            tile = slots.tile([P, C], U8, name="slot_scales", align_bytes=64)
-            nc.vector.tensor_copy(tile[:], x_scales[:].indirect(lst))
-            slot_tiles[e] = (words, tile)
+            scales = slots.tile([P, C], U8, name="slot_scales", align_bytes=64)
+            nc.vector.tensor_copy(scales[:], x_scales[:].indirect(entries))
+            slot_codes[e] = (words, scales)
 
         def first_product(kind, e):
             banks = []
-            words, scales = slot_tiles[e]
-            for half in range(2):
+            words, scales = packed[kind, e]
+            x_words, slot_scales = slot_codes[e]
+            for half in range(HALVES):
                 bank = psum.tile([P, PACK, P], F32, name="bank_a" if kind == "w1" else "bank_b")
                 cols = slice(half * P, (half + 1) * P)
                 for t in range(PACK):
-                    for p in range(PASSES):
-                        c_tile, s_tile = ready[(kind, e, p)]
+                    rows = slice(t * P, (t + 1) * P)
+                    for s in range(PASSES):
                         nc.tensor.matmul_mx(
                             out=bank[:, t, :],
-                            lhsT=c_tile[:, t * P : (t + 1) * P].bitcast(FP8X4),
-                            lhsT_scale=s_tile[:, t * P : (t + 1) * P],
-                            rhs=words[p][:, cols].bitcast(FP8X4),
-                            rhs_scale=scales[4 * p : P, cols],
-                            start=(p == 0),
-                            stop=(p == PASSES - 1),
+                            lhsT=words[:, s, rows].bitcast(FP8X4),
+                            lhsT_scale=scales[:, s, rows],
+                            rhs=x_words[s][:, cols].bitcast(FP8X4),
+                            rhs_scale=slot_scales[SCALE_STEP * s : P, cols],
+                            start=(s == 0),
+                            stop=(s == PASSES - 1),
                         )
                 banks.append(bank)
             return banks
 
-        a_banks, b_banks, moved, h_bf, h_ready, y_banks = {}, {}, {}, {}, {}, {}
+        def take_relu(e):
+            for half in range(HALVES):
+                nc.scalar.activation(
+                    relu_a[e][:, half, :, :], a_banks[e][half][:].rearrange("p t c -> p c t"), RELU
+                )
 
-        def move_a(e):
-            for half in range(2):
-                tile = moved[e][half]
-                nc.scalar.activation(tile, a_banks[e][half][:].rearrange("p t n -> p n t"), RELU)
-
-        def move_b(e):
-            moved[e] = []
-            for half in range(2):
-                tile = hidden.tile([P, P, PACK], F32, name="moved", bufs=3)
-                nc.scalar.copy(tile[:], b_banks[e][half][:].rearrange("p t n -> p n t"))
-                moved[e].append(tile)
-
-        def gated(e):
-            if e in h_bf:
-                tile = h_bf[e]
-            else:
-                tile = hidden.tile([P, C, PACK], BF16, name="h_bf", align_bytes=64, bufs=2)
-            for half in range(2):
+        def take_h(e):
+            if e not in h_bf:
+                h_bf[e] = hidden.tile([P, C, PACK], BF16, name="h_bf", align_bytes=64)
+            for half in range(HALVES):
                 nc.vector.tensor_tensor(
-                    tile[:, half * P : (half + 1) * P, :],
-                    b_banks[e][half][:].rearrange("p t n -> p n t"),
-                    moved[e][half],
+                    h_bf[e][:, half * P : (half + 1) * P, :],
+                    b_banks[e][half][:].rearrange("p t c -> p c t"),
+                    relu_a[e][:, half, :, :],
                     MULT,
                 )
-            h_bf[e] = tile
 
-        def quantise_hidden(e):
-            c_tile = hidden.tile([P, C], U32, name="h_codes", align_bytes=64)
-            s_tile = hidden.tile([P, C], U8, name="h_scales", align_bytes=64)
+        def quantise_h(e):
+            words = hidden_codes.tile([P, C], U32, name="h_codes", align_bytes=64)
+            scales = hidden_codes.tile([P, C], U8, name="h_scales", align_bytes=64)
             nc.vector.quantize_mx(
-                out=c_tile[:].bitcast(FP8X4), scales=s_tile[:], in_=h_bf[e][:].rearrange("p n t -> p (n t)")
+                out=words[:].bitcast(FP8X4), scales=scales[:], in_=h_bf[e][:].rearrange("p c t -> p (c t)")
             )
-            h_ready[e] = (c_tile, s_tile)
+            h_packed[e] = (words, scales)
 
         def second_product(e):
-            c_tile, s_tile = ready[("w2", e, 0)]
-            hc, hs = h_ready[e]
-            bank = psum_y.tile([P, 2, C], F32, name="bank_y")
-            for n in range(2):
+            words, scales = packed["w2", e]
+            h_words, h_scales = h_packed[e]
+            bank = psum_y.tile([P, HALVES, C], F32, name="bank_y")
+            for n in range(HALVES):
+                rows = slice(n * P, (n + 1) * P)
                 nc.tensor.matmul_mx(
                     out=bank[:, n, :],
-                    lhsT=c_tile[:, n * P : (n + 1) * P].bitcast(FP8X4),
-                    lhsT_scale=s_tile[:, n * P : (n + 1) * P],
-                    rhs=hc[:].bitcast(FP8X4),
-                    rhs_scale=hs[:],
+                    lhsT=words[:, rows].bitcast(FP8X4),
+                    lhsT_scale=scales[:, rows],
+                    rhs=h_words[:].bitcast(FP8X4),
+                    rhs_scale=h_scales[:],
                     start=True,
                     stop=True,
                 )
             y_banks[e] = bank
 
-        def copy_y(e):
-            for n in range(2):
+        def copy_y(e, halves):
+            for n in halves:
                 nc.scalar.copy(out=y_sb[n][:, e * C : (e + 1) * C], in_=y_banks[e][:, n, :])
 
-        plan = {}
+        agenda = {}
 
-        def later(step, fn, *args):
-            plan.setdefault(step, []).append((fn, args))
-
-        for g, step in GATHER_STEP.items():
-            later(step, gather, g)
-
-        def after_quantise(step, job):
-            kind, e, p = job
-            if kind == "w1" and p == 1:
-                a_banks[e] = first_product("w1", e)
-            if kind == "w3" and p == 1:
-                move_a(e)
-                while held_y:
-                    copy_y(held_y.pop(0))
-                b_banks[e] = first_product("w3", e)
-                later(step + 2, gated, e)
-                later(step + 2, quantise_hidden, e)
-                later(step + 2, finish, e, step + 2)
-            if kind == "w2":
-                later(step, finish, e, step)
-
-        done, held_y, late_y = [], [], []
+        def put_off(step, action, *args):
+            agenda.setdefault(step, []).append((action, args))
 
         def finish(e, step):
-            if e in h_ready and ("w2", e, 0) in ready and e not in done:
-                done.append(e)
+            if e in h_packed and ("w2", e) in packed and e not in y_banks:
                 second_product(e)
-                if e < 2 and e < E - 1:
-                    held_y.append(e)
-                elif e < E - 1:
-                    late_y.append(e)
+                if e < EARLY_W2:
+                    put_off(max(step, chunks.index(("w3", e + 1, 1))) + 1, copy_y, e, range(HALVES))
                 else:
-                    while late_y:
-                        copy_y(late_y.pop(0))
-                    later(step + 1, copy_y, e)
+                    put_off(max(step, 0 if e == LAST else len(chunks) - 1) + 1, copy_y, e, (0,))
 
-        total = len(jobs)
+        def follow(chunk, step):
+            kind, e, s = chunk
+            if kind == "w1" and s == PASSES - 1:
+                a_banks[e] = first_product(kind, e)
+            if kind == "w3" and s == PASSES - 1:
+                take_relu(e)
+                b_banks[e] = first_product(kind, e)
+                put_off(step + 2, take_h, e)
+                put_off(step + 2, quantise_h, e)
+                put_off(step + 2, finish, e, step + 2)
+            if kind == "w2":
+                put_off(step, finish, e, step)
+
+        for e in range(E):
+            put_off(max(PASSES + 1, 4 * e + 1), gather_tokens, e)
         loaded = 0
-        for step in range(total + 8):
-            while loaded < min(step + AHEAD + 1, total):
-                load(jobs[loaded])
+        step = 0
+        while step <= len(chunks) or agenda:
+            while loaded < min(step + AHEAD + 1, len(chunks)):
+                load(chunks[loaded])
                 loaded += 1
-                if loaded == 6:
+                if loaded == 1:
+                    nc.sync.dma_start(offs_sb[:], offs)
+                if loaded == len(chunks):
                     for r, pos in enumerate((pos1, pos2, pos3)):
                         nc.sync.dma_start(pos_sb[r][:], pos)
-                if loaded == total:
-                    for n in range(2):
-                        for r in range(TOP):
-                            nc.sync.dma_start(out=gate_sb[n][r][:], in_=gate[r, n * P : (n + 1) * P, :])
-            if step < total:
-                group(jobs[step])
-            if 1 <= step < total + 1:
-                quantise(jobs[step - 1])
-                after_quantise(step, jobs[step - 1])
-            for fn, args in plan.get(step, []):
-                fn(*args)
+                    for n in range(HALVES):
+                        rows = slice(n * P, (n + 1) * P)
+                        nc.sync.dma_start(out=gate_sb[n][:], in_=gate[:, rows, :].rearrange("r p t -> p r t"))
+            if step < len(chunks):
+                interleave(chunks[step])
+            if 1 <= step <= len(chunks):
+                quantise(chunks[step - 1])
+                follow(chunks[step - 1], step)
+            for action, args in agenda.pop(step, []):
+                action(*args)
+            step += 1
 
-        for n in range(2):
-            parts = []
-            for r in range(TOP):
-                tile = keep.tile([P, T], F32, name=f"part{n}_{r}")
-                nc.vector.tensor_tensor(tile[:], y_sb[n][:].indirect(pos_sb[r][:]), gate_sb[n][r][:], MULT)
-                parts.append(tile)
-            total01 = keep.tile([P, T], F32, name=f"total01_{n}")
-            nc.vector.tensor_tensor(total01[:], parts[0][:], parts[1][:], ADD)
-            result = keep.tile([P, T], F32, name=f"result{n}")
-            nc.vector.tensor_tensor(result[:], total01[:], parts[2][:], ADD)
-            nc.sync.dma_start(out=out[n * P : (n + 1) * P, :], in_=result[:])
+        nc.scalar.copy(y_sb[1][:, LATE[0] * C : E * C : C], gate_sb[0][:, 0, 0 : E - LATE[0]])
+        for e in LATE:
+            copy_y(e, (1,))
+
+        def fetch(n, r, cols):
+            part = keep.tile([P, cols.stop - cols.start], F32, name=f"part{n}_{r}_{cols.start}")
+            entries = pos_sb[r][:, cols.start // 16 : cols.stop // 16]
+            nc.vector.tensor_tensor(part[:], y_sb[n][:].indirect(entries), gate_sb[n][:, r, cols], MULT)
+            return part
+
+        def add(name, first, second):
+            total = keep.tile([P, second.shape[1]], F32, name=name)
+            nc.vector.tensor_tensor(total[:], first, second[:], ADD)
+            return total
+
+        tokens = slice(0, T)
+        part0 = fetch(0, 0, tokens)
+        part1 = fetch(0, 1, tokens)
+        part2 = fetch(0, 2, tokens)
+        pair = add("pair0", part0[:], part1)
+        next0 = fetch(1, 0, tokens)
+        result = add("result0", pair[:], part2)
+        nc.sync.dma_start(out=out[0:P, :], in_=result[:])
+        next1 = fetch(1, 1, tokens)
+        pair = add("pair1", next0[:], next1)
+        token_halves = [slice(q * T // 2, (q + 1) * T // 2) for q in range(2)]
+        ends = [fetch(1, 2, cols) for cols in token_halves]
+        for cols, end in zip(token_halves, ends):
+            result = add(f"result1_{cols.start}", pair[:, cols], end)
+            nc.sync.dma_start(out=out[P : 2 * P, cols], in_=result[:])

from contextlib import ExitStack

import concourse.mybir as mybir

K, T, E, C, H, N = 1024, 512, 6, 256, 512, 256
TOP = 3
SLOTS = E * C
FLOPS = 2 * SLOTS * (2 * K * H + H * N)

F32 = mybir.dt.float32
BF16 = mybir.dt.bfloat16
U32 = mybir.dt.uint32
U16 = mybir.dt.uint16
U8 = mybir.dt.uint8
FP8X4 = mybir.dt.float8_e4m3fn_x4
MULT = mybir.AluOpType.mult
ADD = mybir.AluOpType.add
RELU = mybir.ActivationFunctionType.Relu

P = 128
PACK = 4
PASS = P * PACK
PASSES = K // PASS
HALVES = 2
QUAD = 4
SCALE_STEP = 4

AHEAD = 7
RAW_BUFS = AHEAD + 2
EARLY_W2 = 2
LATE = range(EARLY_W2, E)
LAST = E - 1
X_QUADS_ON_VECTOR = 64
LAST_W3_QUADS_ON_VECTOR = 32


def chunk_order():
    order = [("x", 0, s) for s in range(PASSES)]
    for e in range(E):
        order += [(kind, e, s) for kind in ("w1", "w3") for s in range(PASSES)]
        if e < EARLY_W2:
            order.append(("w2", e, 0))
    return order + [("w2", e, 0) for e in LATE]


def quads_on_vector(kind, e, s):
    if kind == "x":
        return X_QUADS_ON_VECTOR if s == 0 else 0
    if kind == "w2":
        return N // QUAD if e < EARLY_W2 or e == LAST else 0
    if s == 1:
        return H // QUAD
    return LAST_W3_QUADS_ON_VECTOR if (kind, e) == ("w3", LAST) else 0


def tile_moe_tk_glu_relu_kernel(tc, xT, w1, w3, w2, gate, offs, pos1, pos2, pos3, out):
    nc = tc.nc
    with ExitStack() as ctx:
        keep = ctx.enter_context(tc.tile_pool(name="keep", bufs=1))
        raws = ctx.enter_context(tc.tile_pool(name="raws", bufs=RAW_BUFS))
        raws2 = ctx.enter_context(tc.tile_pool(name="raws2", bufs=4))
        groups = ctx.enter_context(tc.tile_pool(name="groups", bufs=3))
        codes = ctx.enter_context(tc.tile_pool(name="codes", bufs=4))
        codes2 = ctx.enter_context(tc.tile_pool(name="codes2", bufs=E))
        slots = ctx.enter_context(tc.tile_pool(name="slots", bufs=E))
        hidden = ctx.enter_context(tc.tile_pool(name="hidden", bufs=2))
        hidden_codes = ctx.enter_context(tc.tile_pool(name="hidden_codes", bufs=E))
        psum = ctx.enter_context(tc.psum_pool(name="psum", bufs=HALVES))
        psum_y = ctx.enter_context(tc.psum_pool(name="psum_y", bufs=4))

        offs_sb = keep.tile([P, SLOTS // 16], U16, name="offs_sb")
        pos_sb = [keep.tile([P, T // 16], U16, name=f"pos_sb{r}") for r in range(TOP)]
        x_codes = [keep.tile([P, T], U32, name=f"x_codes{s}", align_bytes=64) for s in range(PASSES)]
        x_scales = keep.tile([P, T], U8, name="x_scales", align_bytes=64)
        nc.gpsimd.memset(x_scales[:], 0)
        y_sb = [keep.tile([P, SLOTS], F32, name=f"y_sb{n}") for n in range(HALVES)]
        gate_sb = [keep.tile([P, TOP, T], F32, name=f"gate_sb{n}") for n in range(HALVES)]

        chunks = chunk_order()
        raw, grouped, packed = {}, {}, {}
        slot_codes, relu_a, h_bf, h_packed = {}, {}, {}, {}
        a_banks, b_banks, y_banks = {}, {}, {}

        def load(chunk):
            kind, e, s = chunk
            if kind == "w2":
                tile = raws2.tile([P, PACK, N], F32, name="raw2")
                rows = w2[e]
            else:
                tile = raws.tile([P, PACK, PASS], F32, name="raw")
                rows = {"x": xT, "w1": w1[e], "w3": w3[e]}[kind][s * PASS : (s + 1) * PASS, :]
            nc.sync.dma_start(out=tile[:], in_=rows.rearrange("(p j) w -> p j w", j=PACK))
            raw[chunk] = tile

        def interleave(chunk):
            kind, e, s = chunk
            tile = raw.pop(chunk)
            if kind == "w2":
                target = groups.tile([P, PACK * N], BF16, name="grouped2", align_bytes=64)
                flat = target[:]
            else:
                if s == 0:
                    target = groups.tile([P, PASSES, PACK * PASS], BF16, name="grouped", align_bytes=64)
                else:
                    target = grouped[kind, e, 0]
                flat = target[:, s, :]
            grouped[chunk] = target
            source = tile[:].rearrange("p j (m i) -> p m j i", i=QUAD)
            if kind in ("w1", "w3"):
                flat = flat.rearrange("p (i m j) -> p m j i", i=QUAD, j=PACK)
            else:
                flat = flat.rearrange("p (m i j) -> p m j i", i=QUAD, j=PACK)

            if kind == "w1" and s == 1 and e > 0:
                h_bf[e - 1] = hidden.tile([P, C, PACK], BF16, name="h_bf", align_bytes=64)
                nc.vector.tensor_copy(h_bf[e - 1][:, 0:C:P, 0:2], tile[:, 0:2, 0:2])
            cut = quads_on_vector(kind, e, s)
            if cut > 0:
                nc.vector.tensor_copy(out=flat[:, :cut], in_=source[:, :cut])
            if cut < source.shape[1]:
                nc.scalar.copy(out=flat[:, cut:], in_=source[:, cut:])
            if kind == "w3" and s == 1:
                relu_a[e] = hidden.tile([P, HALVES, P, PACK], F32, name="relu_a")
                nc.scalar.copy(relu_a[e][:, :, 0, 0], tile[:, 0:HALVES, 0])
                if 1 <= e <= EARLY_W2:
                    for n in range(HALVES):
                        nc.scalar.copy(y_sb[n][:, (e - 1) * C : (e - 1) * C + 1], tile[:, 0, 0:1])
            if chunk == chunks[-1]:
                nc.scalar.copy(y_sb[0][:, LATE[0] * C : LAST * C : C], tile[:, 0, 0 : LAST - LATE[0]])

        def quantise(chunk):
            kind, e, s = chunk
            source = grouped[chunk]
            if kind == "x":
                nc.vector.quantize_mx(
                    out=x_codes[s][:].bitcast(FP8X4), scales=x_scales[SCALE_STEP * s : P, :], in_=source[:, s, :]
                )
                return
            if kind == "w2":
                words = codes2.tile([P, N], U32, name="w2_codes", align_bytes=64)
                scales = codes2.tile([P, N], U8, name="w2_scales", align_bytes=64)
                nc.vector.quantize_mx(out=words[:].bitcast(FP8X4), scales=scales[:], in_=source[:])
                packed[kind, e] = (words, scales)
                return
            if s == 0:
                words = codes.tile([P, PASSES, H], U32, name="w_codes", align_bytes=64)
                scales = codes.tile([P, PASSES, H], U8, name="w_scales", align_bytes=64)
                packed[kind, e] = (words, scales)
            words, scales = packed[kind, e]
            if (kind, e) == ("w3", LAST):
                nc.vector.quantize_mx(out=words[:, s, :].bitcast(FP8X4), scales=scales[:, s, :], in_=source[:, s, :])
            elif s == PASSES - 1:
                nc.vector.quantize_mx(
                    out=words[:].rearrange("p s w -> p (s w)").bitcast(FP8X4),
                    scales=scales[:].rearrange("p s w -> p (s w)"),
                    in_=source[:].rearrange("p s w -> p (s w)"),
                )

        def gather_tokens(e):
            entries = offs_sb[:, e * C // 16 : (e + 1) * C // 16]
            words = []
            for s in range(PASSES):
                tile = slots.tile([P, C], U32, name=f"slot_codes{s}", align_bytes=64)
                nc.vector.tensor_copy(tile[:], x_codes[s][:].indirect(entries))
                words.append(tile)
            scales = slots.tile([P, C], U8, name="slot_scales", align_bytes=64)
            nc.vector.tensor_copy(scales[:], x_scales[:].indirect(entries))
            slot_codes[e] = (words, scales)

        def first_product(kind, e):
            banks = []
            words, scales = packed[kind, e]
            x_words, slot_scales = slot_codes[e]
            for half in range(HALVES):
                bank = psum.tile([P, PACK, P], F32, name="bank_a" if kind == "w1" else "bank_b")
                cols = slice(half * P, (half + 1) * P)
                for t in range(PACK):
                    rows = slice(t * P, (t + 1) * P)
                    for s in range(PASSES):
                        nc.tensor.matmul_mx(
                            out=bank[:, t, :],
                            lhsT=words[:, s, rows].bitcast(FP8X4),
                            lhsT_scale=scales[:, s, rows],
                            rhs=x_words[s][:, cols].bitcast(FP8X4),
                            rhs_scale=slot_scales[SCALE_STEP * s : P, cols],
                            start=(s == 0),
                            stop=(s == PASSES - 1),
                        )
                banks.append(bank)
            return banks

        def take_relu(e):
            for half in range(HALVES):
                nc.scalar.activation(
                    relu_a[e][:, half, :, :], a_banks[e][half][:].rearrange("p t c -> p c t"), RELU
                )

        def take_h(e):
            if e not in h_bf:
                h_bf[e] = hidden.tile([P, C, PACK], BF16, name="h_bf", align_bytes=64)
            for half in range(HALVES):
                nc.vector.tensor_tensor(
                    h_bf[e][:, half * P : (half + 1) * P, :],
                    b_banks[e][half][:].rearrange("p t c -> p c t"),
                    relu_a[e][:, half, :, :],
                    MULT,
                )

        def quantise_h(e):
            words = hidden_codes.tile([P, C], U32, name="h_codes", align_bytes=64)
            scales = hidden_codes.tile([P, C], U8, name="h_scales", align_bytes=64)
            nc.vector.quantize_mx(
                out=words[:].bitcast(FP8X4), scales=scales[:], in_=h_bf[e][:].rearrange("p c t -> p (c t)")
            )
            h_packed[e] = (words, scales)

        def second_product(e):
            words, scales = packed["w2", e]
            h_words, h_scales = h_packed[e]
            bank = psum_y.tile([P, HALVES, C], F32, name="bank_y")
            for n in range(HALVES):
                rows = slice(n * P, (n + 1) * P)
                nc.tensor.matmul_mx(
                    out=bank[:, n, :],
                    lhsT=words[:, rows].bitcast(FP8X4),
                    lhsT_scale=scales[:, rows],
                    rhs=h_words[:].bitcast(FP8X4),
                    rhs_scale=h_scales[:],
                    start=True,
                    stop=True,
                )
            y_banks[e] = bank

        def copy_y(e, halves):
            for n in halves:
                nc.scalar.copy(out=y_sb[n][:, e * C : (e + 1) * C], in_=y_banks[e][:, n, :])

        agenda = {}

        def put_off(step, action, *args):
            agenda.setdefault(step, []).append((action, args))

        def finish(e, step):
            if e in h_packed and ("w2", e) in packed and e not in y_banks:
                second_product(e)
                if e < EARLY_W2:
                    put_off(max(step, chunks.index(("w3", e + 1, 1))) + 1, copy_y, e, range(HALVES))
                else:
                    put_off(max(step, 0 if e == LAST else len(chunks) - 1) + 1, copy_y, e, (0,))

        def follow(chunk, step):
            kind, e, s = chunk
            if kind == "w1" and s == PASSES - 1:
                a_banks[e] = first_product(kind, e)
            if kind == "w3" and s == PASSES - 1:
                take_relu(e)
                b_banks[e] = first_product(kind, e)
                put_off(step + 2, take_h, e)
                put_off(step + 2, quantise_h, e)
                put_off(step + 2, finish, e, step + 2)
            if kind == "w2":
                put_off(step, finish, e, step)

        for e in range(E):
            put_off(max(PASSES + 1, 4 * e + 1), gather_tokens, e)
        loaded = 0
        step = 0
        while step <= len(chunks) or agenda:
            while loaded < min(step + AHEAD + 1, len(chunks)):
                load(chunks[loaded])
                loaded += 1
                if loaded == 1:
                    nc.sync.dma_start(offs_sb[:], offs)
                if loaded == len(chunks):
                    for r, pos in enumerate((pos1, pos2, pos3)):
                        nc.sync.dma_start(pos_sb[r][:], pos)
                    for n in range(HALVES):
                        rows = slice(n * P, (n + 1) * P)
                        nc.sync.dma_start(out=gate_sb[n][:], in_=gate[:, rows, :].rearrange("r p t -> p r t"))
            if step < len(chunks):
                interleave(chunks[step])
            if 1 <= step <= len(chunks):
                quantise(chunks[step - 1])
                follow(chunks[step - 1], step)
            for action, args in agenda.pop(step, []):
                action(*args)
            step += 1

        nc.scalar.copy(y_sb[1][:, LATE[0] * C : E * C : C], gate_sb[0][:, 0, 0 : E - LATE[0]])
        for e in LATE:
            copy_y(e, (1,))

        def fetch(n, r, cols):
            part = keep.tile([P, cols.stop - cols.start], F32, name=f"part{n}_{r}_{cols.start}")
            entries = pos_sb[r][:, cols.start // 16 : cols.stop // 16]
            nc.vector.tensor_tensor(part[:], y_sb[n][:].indirect(entries), gate_sb[n][:, r, cols], MULT)
            return part

        def add(name, first, second):
            total = keep.tile([P, second.shape[1]], F32, name=name)
            nc.vector.tensor_tensor(total[:], first, second[:], ADD)
            return total

        tokens = slice(0, T)
        part0 = fetch(0, 0, tokens)
        part1 = fetch(0, 1, tokens)
        part2 = fetch(0, 2, tokens)
        pair = add("pair0", part0[:], part1)
        next0 = fetch(1, 0, tokens)
        result = add("result0", pair[:], part2)
        nc.sync.dma_start(out=out[0:P, :], in_=result[:])
        next1 = fetch(1, 1, tokens)
        pair = add("pair1", next0[:], next1)
        token_halves = [slice(q * T // 2, (q + 1) * T // 2) for q in range(2)]
        ends = [fetch(1, 2, cols) for cols in token_halves]
        for cols, end in zip(token_halves, ends):
            result = add(f"result1_{cols.start}", pair[:, cols], end)
            nc.sync.dma_start(out=out[P : 2 * P, cols], in_=result[:])
